import numpy as np, ml_dtypes
CORES = [9,10,11,14,17,18,19,22,49,50,51,54]
N = 12
KB, QP = 2, 32
ROOT = 7
def setup_inputs(rng):
    q = rng.standard_normal((N, 128, QP), dtype=np.float32) / 4; k = rng.standard_normal((N, 128, KB * 128), dtype=np.float32)
    a = 2 * np.pi * rng.random((N, QP)); s = 400 * rng.random((N, QP)) ** 1.5; q[:, 0, :] = s * np.cos(a); q[:, 1, :] = s * np.sin(a); q[:, 2, :] = 150 * rng.standard_normal((N, QP)); k[:, 2, :] = 1 + k[:, 2, :] / 50
    a = (2 * np.pi * rng.random() + np.pi / 2 * (rng.permutation(N).reshape(N, 1, 1) + 0.5) / N - 0.5 + (np.arange(KB).reshape(1, KB, 1) + rng.random((N, KB, 128))) / KB).reshape(N, KB * 128); k[:, 0, :] = np.cos(a); k[:, 1, :] = np.sin(a)
    for t in range(0, QP, 2):
        j, i = (t // 2) % N, rng.integers(KB * 128); q[ROOT, :2, t] = s[ROOT, t] * k[j, :2, i]; q[ROOT, 3:, t] += k[j, 3:, i] / 8
    return {"q": q.astype(ml_dtypes.bfloat16), "k": k.astype(ml_dtypes.bfloat16), "v": rng.standard_normal((N, 128, KB * 128), dtype=np.float32).astype(ml_dtypes.bfloat16)}
def setup_inputs_big(rng):
    d = setup_inputs(rng)
    for k in ("v",): d[k] = (d[k].astype(np.float32) * 1048576.0).astype(d[k].dtype)
    return d
def setup_inputs_small(rng):
    d = setup_inputs(rng)
    for k in ("v",): d[k] = (d[k].astype(np.float32) * (1 / 1048576.0)).astype(d[k].dtype)
    return d
def reference(q, k, v):
    Q, K, V = q.astype(np.float64), k.astype(np.float64), v.astype(np.float64)
    y = np.full((N, QP, 128), np.nan)
    for r in [ROOT]:
        js = list(range(N))
        S = np.concatenate([K[j].T @ Q[r] for j in js], axis=0)
        P = np.exp(S - S.max(axis=0)); P = P / P.sum(axis=0)
        y[r] = P.T @ np.concatenate([V[j][:, 128 * b:128 * b + 128] for j in js for b in range(KB)], axis=0)
    return {"y": y.astype(ml_dtypes.bfloat16)}

@@ -1,0 +1,238 @@
+from concourse.bass import DstId, RemoteDMATransfer
+from concourse.mybir import AluOpType, AxisListType, ActivationFunctionType
+
+NSIM = 64
+NR = 12
+QP = 32
+SLOT = 40
+PAY = 34
+NE_Q = 8
+NE_P = 8
+NE_KV = 16
+
+SCRATCH = {
+    "qd": ("dram", [128, QP], "bfloat16"),
+    "qz": ("sbuf", [128, 3 * QP], "bfloat16"),
+    "kv": ("sbuf", [128, 512], "bfloat16"),
+    "zero": ("sbuf", [128, 128], "bfloat16"),
+    "ones": ("sbuf", [128, 128], "bfloat16"),
+    "e4": ("sbuf", [128, 128], "bfloat16"),
+    "negm": ("sbuf", [128, 8], "bfloat16"),
+    "diag2": ("sbuf", [128, 2 * QP], "bfloat16"),
+    "p": ("sbuf", [128, 2 * QP], "bfloat16"),
+    "stg": ("sbuf", [128, 64], "bfloat16"),
+    "send": ("sbuf", [128, 72], "bfloat16"),
+    "land": ("sbuf", [128, NR * SLOT], "bfloat16"),
+    "ident": ("sbuf", [128, 128], "bfloat16"),
+    "nM": ("sbuf", [128, 4], "float32"),
+    "w": ("sbuf", [128, NR], "float32"),
+    "prod": ("sbuf", [128, NR * 33], "bfloat16"),
+    "hb": ("sbuf", [128, 36], "float32"),
+    "tot": ("sbuf", [128, 36], "float32"),
+    "rL": ("sbuf", [128, 4], "float32"),
+    "ysb": ("sbuf", [128, QP], "bfloat16"),
+    "ps_st": ("psum", [128, 512], "float32"),
+    "ps_s": ("psum", [128, 512], "float32"),
+    "ps_m": ("psum", [128, 512], "float32"),
+    "ps_o": ("psum", [128, 512], "float32"),
+    "ps_y": ("psum", [128, 512], "float32"),
+}
+SEMAPHORES = ["qstage", "qsent", "qarr", "qload", "kload", "vload", "kvarr", "sent", "arrived",
+              "c_zero", "c_marg", "c_ones", "c_e4", "c_id",
+              "s_st", "s_m", "s_d", "s_mr", "s_x", "s_s", "s_p", "s_o", "s_g", "s_t",
+              "r1", "r2", "r3d", "r3a", "r4", "r5", "r6", "r7", "r8", "yd_s", "yd_a"]
+
+EXP = ActivationFunctionType.Exp
+COPY = ActivationFunctionType.Copy
+
+
+def _engines(mask, n):
+    out, k, b = 0, 0, 0
+    while k < n:
+        if (mask >> b) & 1:
+            out |= 1 << b
+            k += 1
+        b += 1
+    return out
+
+
+def _plan(T, topo):
+    root = T.cores[T.root]
+    taken = set(T.cores)
+    workers, feeds = [], {}
+    for c in T.cores:
+        if c == root or topo.may_write(c, root):
+            workers.append(c)
+            continue
+        h = [x for x in range(NSIM)
+             if x not in taken and topo.chip(x) == topo.chip(c) and topo.may_write(x, root)][0]
+        taken.add(h)
+        workers.append(h)
+        feeds[c] = h
+    return root, workers, feeds
+
+
+def _distance(topo, a, b):
+    ca, cb = topo.chip(a), topo.chip(b)
+    if ca == cb:
+        return 2
+    if topo.same_plane(ca, cb) or topo.mates(ca, cb):
+        return 1
+    return 0
+
+
+def rank_program(g, core, T, topo):
+    root, workers, feeds = _plan(T, topo)
+    S = T.sem
+    dve, act, pe, sy = g.vector, g.scalar, g.tensor, g.sync
+
+    if core in feeds:
+        h = feeds[core]
+        sy.dma_start(T.kv[:, 0:256], T.k[:, :]).then_inc(S.kload, 16)
+        act.dma_start(T.kv[:, 256:512], T.v[:, :]).then_inc(S.vload, 16)
+        g.wait_ge(S.kload, 16)
+        g.wait_ge(S.vload, 16)
+        rid, pid, _ = topo.addr(h)
+        g.remote_dma(T.kv[:, :], T.kv[:, :], S.kvarr, S.sent, pid, rid, _engines(topo.mask(core, h), NE_KV))
+        g.wait_ge(S.sent, NE_KV)
+        return
+    if core not in workers:
+        return
+
+    slot = workers.index(core)
+    is_root = core == root
+    fed = core in feeds.values()
+
+    dve.memset(T.zero[:, :], 0.0).then_inc(S.c_zero, 1)
+    dve.memset(T.qz[:, 0:QP], 0.0).then_inc(S.c_marg, 1)
+    dve.memset(T.qz[:, 2 * QP:3 * QP], 0.0).then_inc(S.c_marg, 1)
+
+    if is_root:
+        sy.dma_start(T.qd[:, :], T.q[:, :]).then_inc(S.qstage, 16)
+        others = sorted([w for w in workers if w != root], key=lambda w: _distance(topo, root, w))
+        m = topo.mask(root, others[0])
+        for w in others:
+            m &= topo.mask(root, w)
+        g.wait_ge(S.qstage, 16)
+        g.remote_dma_fused([RemoteDMATransfer(
+            dst_ids=[DstId(rid=topo.addr(w)[0], pnc=topo.addr(w)[1]) for w in others],
+            dma_engine_mask=_engines(m, NE_Q), remote_sem=S.qarr,
+            srcs=[T.qd[:, :]], dsts=[T.qd[:, :] for w in others], alu_op=0)], local_sem=S.qsent)
+        act.wait_ge(S.c_zero, 1)
+        act.activation(T.ones[:, :], T.zero[:, :], EXP).then_inc(S.c_ones, 1)
+        sy.wait_ge(S.qsent, NE_Q)
+        sy.dma_start(T.kv[:, 0:256], T.k[:, :]).then_inc(S.kload, 16)
+        act.wait_ge(S.qsent, NE_Q)
+        act.dma_start(T.qz[:, QP:2 * QP], T.q[:, :]).then_inc(S.qload, 16)
+        act.dma_start(T.kv[:, 256:512], T.v[:, :]).then_inc(S.vload, 16)
+    else:
+        if not fed:
+            sy.dma_start(T.kv[:, 0:256], T.k[:, :]).then_inc(S.kload, 16)
+            act.dma_start(T.kv[:, 256:512], T.v[:, :]).then_inc(S.vload, 16)
+        act.wait_ge(S.c_zero, 1)
+        act.activation(T.ones[:, :], T.zero[:, :], EXP).then_inc(S.c_ones, 1)
+        sy.wait_ge(S.qarr, NE_Q)
+        sy.dma_start(T.qz[:, QP:2 * QP], T.qd[:, :]).then_inc(S.qload, 16)
+
+    g.wait_ge(S.c_ones, 1)
+    g.affine_select(T.e4[0:32, :], T.ones[0:32, :], [[0, 4], [-1, 32]], AluOpType.is_equal, 0.0, 0, 1
+                    ).then_inc(S.c_e4, 1)
+    if is_root:
+        g.affine_select(T.ident[:, :], T.ones[:, :], [[-1, 128]], AluOpType.is_equal, 0.0, 0, 1
+                        ).then_inc(S.c_id, 1)
+
+    if fed:
+        pe.wait_ge(S.kvarr, NE_KV)
+    else:
+        pe.wait_ge(S.kload, 16)
+    pe.wait_ge(S.qload, 16)
+    pe.wait_ge(S.c_marg, 2)
+    pe.matmul(T.ps_st[0:32, 0:256], T.qz[:, QP:2 * QP], T.kv[:, 0:256], True, True).then_inc(S.s_st, 1)
+    pe.matmul(T.ps_s[:, 0:64], T.kv[:, 0:128], T.qz[:, QP:3 * QP], True, False)
+    pe.matmul(T.ps_s[:, 0:64], T.kv[:, 128:256], T.qz[:, 0:2 * QP], False, False)
+
+    dve.wait_ge(S.s_st, 1)
+    dve.tensor_reduce(T.negm[0:32, 0:1], T.ps_st[0:32, 0:256], AxisListType.X, AluOpType.max, negate=True
+                      ).then_inc(S.s_m, 1)
+    dve.wait_ge(S.s_m, 1)
+    dve.wait_ge(S.c_e4, 1)
+    dve.tensor_scalar(T.diag2[0:32, :], T.e4[0:32, 0:64], T.negm[0:32, 0:1], None, AluOpType.mult
+                      ).then_inc(S.s_d, 1)
+
+    pe.wait_ge(S.c_e4, 1)
+    pe.wait_ge(S.s_m, 1)
+    pe.matmul(T.ps_m[:, 0:1], T.e4[0:32, :], T.negm[0:32, 0:1], True, True).then_inc(S.s_mr, 1)
+    pe.wait_ge(S.c_ones, 1)
+    pe.wait_ge(S.s_d, 1)
+    pe.matmul(T.ps_s[:, 0:64], T.ones[0:32, :], T.diag2[0:32, :], False, True).then_inc(S.s_s, 1)
+
+    dve.wait_ge(S.s_mr, 1)
+    mdst = T.land[:, slot * SLOT:slot * SLOT + 1] if is_root else T.send[:, 7:8]
+    dve.tensor_copy(mdst, T.ps_m[:, 0:1]).then_inc(S.s_x, 1)
+
+    act.wait_ge(S.s_s, 1)
+    act.activation(T.p[:, :], T.ps_s[:, 0:64], EXP).then_inc(S.s_p, 1)
+
+    pe.wait_ge(S.s_p, 1)
+    if not fed:
+        pe.wait_ge(S.vload, 16)
+    pe.matmul(T.ps_o[:, 0:32], T.kv[:, 256:384], T.p[:, 0:32], True, False)
+    pe.matmul(T.ps_o[:, 0:32], T.kv[:, 384:512], T.p[:, 32:64], False, True).then_inc(S.s_o, 1)
+    pe.matmul(T.ps_o[:, 32:64], T.ones[:, :], T.p[:, 0:32], True, False)
+    pe.matmul(T.ps_o[:, 32:64], T.ones[:, :], T.p[:, 32:64], False, True).then_inc(S.s_o, 1)
+
+    dve.wait_ge(S.s_o, 2)
+    dve.tensor_copy(T.stg[:, :], T.ps_o[:, 0:64]).then_inc(S.s_g, 1)
+    dve.wait_ge(S.s_g, 1)
+    dve.transpose(T.send[:, 8:72], T.stg[:, :]).then_inc(S.s_t, 1)
+
+    if not is_root:
+        g.wait_ge(S.s_x, 1)
+        g.wait_ge(S.s_t, 1)
+        rid, pid, _ = topo.addr(root)
+        g.remote_dma(T.land[:, slot * SLOT:slot * SLOT + PAY], T.send[:, 7:7 + PAY], S.arrived, S.sent, pid, rid,
+                     _engines(topo.mask(core, root), NE_P))
+        g.wait_ge(S.sent, NE_P)
+        return
+
+    total = NE_P * (NR - 1)
+    mview = T.land[:, 0:NR * SLOT:SLOT]
+    dve.wait_ge(S.s_t, 1)
+    dve.wait_ge(S.s_x, 1)
+    dve.wait_ge(S.arrived, total)
+    dve.tensor_reduce(T.nM[:, 0:1], mview, AxisListType.X, AluOpType.min).then_inc(S.r1, 1)
+    act.wait_ge(S.arrived, total)
+    act.wait_ge(S.s_x, 1)
+    act.wait_ge(S.s_t, 1)
+    act.wait_ge(S.r1, 1)
+    act.activation(T.w[:, :], mview, EXP, bias=T.nM[:, 0:1], scale=-1.0).then_inc(S.r2, 1)
+    dve.wait_ge(S.r2, 1)
+    act.wait_ge(S.r2, 1)
+    pe.wait_ge(S.c_id, 1)
+    for i in range(NR // 2):
+        for j in (2 * i, 2 * i + 1):
+            src = T.send[:, 8:41] if j == slot else T.land[:, j * SLOT + 1:j * SLOT + PAY]
+            dst = T.prod[:, 33 * j:33 * j + 33]
+            if j % 2 == 0:
+                dve.tensor_scalar(dst, src, T.w[:, j:j + 1], None, AluOpType.mult).then_inc(S.r3d, 1)
+            else:
+                act.activation(dst, src, COPY, scale=T.w[:, j:j + 1]).then_inc(S.r3a, 1)
+        pe.wait_ge(S.r3d, i + 1)
+        pe.wait_ge(S.r3a, i + 1)
+        mm = pe.matmul(T.ps_y[:, 0:66], T.ident[:, :], T.prod[:, 66 * i:66 * i + 66], i == 0, i == NR // 2 - 1)
+    mm.then_inc(S.r4, 1)
+    act.wait_ge(S.r4, 1)
+    act.activation(T.hb[:, 0:33], T.ps_y[:, 33:66], COPY).then_inc(S.r5, 1)
+    dve.wait_ge(S.r5, 1)
+    dve.tensor_tensor(T.tot[:, 0:33], T.ps_y[:, 0:33], T.hb[:, 0:33], AluOpType.add).then_inc(S.r6, 1)
+    dve.wait_ge(S.r6, 1)
+    dve.reciprocal(T.rL[:, 0:1], T.tot[:, 32:33]).then_inc(S.r7, 1)
+    dve.wait_ge(S.r7, 1)
+    dve.tensor_scalar(T.ysb[:, :], T.tot[:, 0:32], T.rL[:, 0:1], None, AluOpType.mult).then_inc(S.r8, 1)
+    sy.wait_ge(S.r8, 1)
+    act.wait_ge(S.r8, 1)
+    for c in range(4):
+        q_, s_ = (sy, S.yd_s) if c % 2 == 0 else (act, S.yd_a)
+        q_.dma_start(T.y[:, 32 * c:32 * c + 32], T.ysb[32 * c:32 * c + 32, :]).then_inc(s_, 16)
+    sy.wait_ge(S.yd_s, 32)
+    act.wait_ge(S.yd_a, 32)

@@ -5,10 +5,12 @@ NSIM = 64
 NR = 12
 QP = 32
 SLOT = 40
-PAY = 34
+PAY = 33
+MS = 8
 NE_Q = 8
+NE_QC = 4
 NE_P = 8
-NE_KV = 16
+NE_KV = 8
 
 SCRATCH = {
     "qd": ("dram", [128, QP], "bfloat16"),
@@ -17,18 +19,17 @@ SCRATCH = {
     "zero": ("sbuf", [128, 128], "bfloat16"),
     "ones": ("sbuf", [128, 128], "bfloat16"),
     "e4": ("sbuf", [128, 128], "bfloat16"),
-    "negm": ("sbuf", [128, 8], "bfloat16"),
+    "negm": ("sbuf", [128, MS], "bfloat16"),
     "diag2": ("sbuf", [128, 2 * QP], "bfloat16"),
     "p": ("sbuf", [128, 2 * QP], "bfloat16"),
     "stg": ("sbuf", [128, 64], "bfloat16"),
-    "send": ("sbuf", [128, 72], "bfloat16"),
+    "send": ("sbuf", [128, 64], "bfloat16"),
+    "mland": ("sbuf", [128, NR * MS], "bfloat16"),
     "land": ("sbuf", [128, NR * SLOT], "bfloat16"),
     "ident": ("sbuf", [128, 128], "bfloat16"),
+    "dg": ("sbuf", [128, NR * 128], "bfloat16"),
     "nM": ("sbuf", [128, 4], "float32"),
     "w": ("sbuf", [128, NR], "float32"),
-    "prod": ("sbuf", [128, NR * 33], "bfloat16"),
-    "hb": ("sbuf", [128, 36], "float32"),
-    "tot": ("sbuf", [128, 36], "float32"),
     "rL": ("sbuf", [128, 4], "float32"),
     "ysb": ("sbuf", [128, QP], "bfloat16"),
     "ps_st": ("psum", [128, 512], "float32"),
@@ -37,10 +38,10 @@ SCRATCH = {
     "ps_o": ("psum", [128, 512], "float32"),
     "ps_y": ("psum", [128, 512], "float32"),
 }
-SEMAPHORES = ["qstage", "qsent", "qarr", "qload", "kload", "vload", "kvarr", "sent", "arrived",
+SEMAPHORES = ["qstage", "qsent", "qarr", "qload", "kload", "vload", "karr", "varr", "sent", "marr", "arrived",
               "c_zero", "c_marg", "c_ones", "c_e4", "c_id",
-              "s_st", "s_m", "s_d", "s_mr", "s_x", "s_s", "s_p", "s_o", "s_g", "s_t",
-              "r1", "r2", "r3d", "r3a", "r4", "r5", "r6", "r7", "r8", "yd_s", "yd_a"]
+              "s_st", "s_m", "s_d", "s_s", "s_p", "s_o", "s_g", "s_t",
+              "r0", "r1", "r2", "r3d", "r3a", "r4", "r7", "r8", "yd_s", "yd_a"]
 
 EXP = ActivationFunctionType.Exp
 COPY = ActivationFunctionType.Copy
@@ -72,13 +73,8 @@ def _plan(T, topo):
     return root, workers, feeds
 
 
-def _distance(topo, a, b):
-    ca, cb = topo.chip(a), topo.chip(b)
-    if ca == cb:
-        return 2
-    if topo.same_plane(ca, cb) or topo.mates(ca, cb):
-        return 1
-    return 0
+def _one_link(topo, a, b):
+    return topo.same_plane(topo.chip(a), topo.chip(b)) or topo.mates(topo.chip(a), topo.chip(b))
 
 
 def rank_program(g, core, T, topo):
@@ -90,11 +86,13 @@ def rank_program(g, core, T, topo):
         h = feeds[core]
         sy.dma_start(T.kv[:, 0:256], T.k[:, :]).then_inc(S.kload, 16)
         act.dma_start(T.kv[:, 256:512], T.v[:, :]).then_inc(S.vload, 16)
-        g.wait_ge(S.kload, 16)
-        g.wait_ge(S.vload, 16)
         rid, pid, _ = topo.addr(h)
-        g.remote_dma(T.kv[:, :], T.kv[:, :], S.kvarr, S.sent, pid, rid, _engines(topo.mask(core, h), NE_KV))
-        g.wait_ge(S.sent, NE_KV)
+        em = _engines(topo.mask(core, h), NE_KV)
+        g.wait_ge(S.kload, 16)
+        g.remote_dma(T.kv[:, 0:256], T.kv[:, 0:256], S.karr, S.sent, pid, rid, em)
+        g.wait_ge(S.vload, 16)
+        g.remote_dma(T.kv[:, 256:512], T.kv[:, 256:512], S.varr, S.sent, pid, rid, em)
+        g.wait_ge(S.sent, 2 * NE_KV)
         return
     if core not in workers:
         return
@@ -102,27 +100,33 @@ def rank_program(g, core, T, topo):
     slot = workers.index(core)
     is_root = core == root
     fed = core in feeds.values()
+    near = topo.chip(core) == topo.chip(root)
 
     dve.memset(T.zero[:, :], 0.0).then_inc(S.c_zero, 1)
     dve.memset(T.qz[:, 0:QP], 0.0).then_inc(S.c_marg, 1)
     dve.memset(T.qz[:, 2 * QP:3 * QP], 0.0).then_inc(S.c_marg, 1)
+    dve.memset(T.negm[:, :], 0.0).then_inc(S.c_marg, 1)
 
     if is_root:
         sy.dma_start(T.qd[:, :], T.q[:, :]).then_inc(S.qstage, 16)
-        others = sorted([w for w in workers if w != root], key=lambda w: _distance(topo, root, w))
-        m = topo.mask(root, others[0])
-        for w in others:
-            m &= topo.mask(root, w)
+        far_w = sorted([w for w in workers if topo.chip(w) != topo.chip(root)], key=lambda w: _one_link(topo, root, w))
+        near_w = [w for w in workers if w != root and topo.chip(w) == topo.chip(root)]
+        m_far = topo.mask(root, far_w[0])
+        for w in far_w:
+            m_far &= topo.mask(root, w)
+        m_far = _engines(m_far, NE_Q)
+        m_near = _engines(topo.mask(root, near_w[0]) & ~m_far, NE_QC)
         g.wait_ge(S.qstage, 16)
         g.remote_dma_fused([RemoteDMATransfer(
-            dst_ids=[DstId(rid=topo.addr(w)[0], pnc=topo.addr(w)[1]) for w in others],
-            dma_engine_mask=_engines(m, NE_Q), remote_sem=S.qarr,
-            srcs=[T.qd[:, :]], dsts=[T.qd[:, :] for w in others], alu_op=0)], local_sem=S.qsent)
+            dst_ids=[DstId(rid=topo.addr(w)[0], pnc=topo.addr(w)[1]) for w in ws],
+            dma_engine_mask=m, remote_sem=S.qarr,
+            srcs=[T.qd[:, :]], dsts=[T.qz[:, QP:2 * QP] for w in ws], alu_op=0)
+            for ws, m in ((far_w, m_far), (near_w, m_near))], local_sem=S.qsent)
         act.wait_ge(S.c_zero, 1)
         act.activation(T.ones[:, :], T.zero[:, :], EXP).then_inc(S.c_ones, 1)
-        sy.wait_ge(S.qsent, NE_Q)
+        sy.wait_ge(S.qsent, NE_Q + NE_QC)
         sy.dma_start(T.kv[:, 0:256], T.k[:, :]).then_inc(S.kload, 16)
-        act.wait_ge(S.qsent, NE_Q)
+        act.wait_ge(S.qsent, NE_Q + NE_QC)
         act.dma_start(T.qz[:, QP:2 * QP], T.q[:, :]).then_inc(S.qload, 16)
         act.dma_start(T.kv[:, 256:512], T.v[:, :]).then_inc(S.vload, 16)
     else:
@@ -131,8 +135,6 @@ def rank_program(g, core, T, topo):
             act.dma_start(T.kv[:, 256:512], T.v[:, :]).then_inc(S.vload, 16)
         act.wait_ge(S.c_zero, 1)
         act.activation(T.ones[:, :], T.zero[:, :], EXP).then_inc(S.c_ones, 1)
-        sy.wait_ge(S.qarr, NE_Q)
-        sy.dma_start(T.qz[:, QP:2 * QP], T.qd[:, :]).then_inc(S.qload, 16)
 
     g.wait_ge(S.c_ones, 1)
     g.affine_select(T.e4[0:32, :], T.ones[0:32, :], [[0, 4], [-1, 32]], AluOpType.is_equal, 0.0, 0, 1
@@ -141,40 +143,44 @@ def rank_program(g, core, T, topo):
         g.affine_select(T.ident[:, :], T.ones[:, :], [[-1, 128]], AluOpType.is_equal, 0.0, 0, 1
                         ).then_inc(S.c_id, 1)
 
+    negm = T.mland[0:32, MS * slot:MS * slot + 1] if is_root else T.negm[0:32, 0:1]
     if fed:
-        pe.wait_ge(S.kvarr, NE_KV)
+        pe.wait_ge(S.karr, NE_KV)
     else:
         pe.wait_ge(S.kload, 16)
-    pe.wait_ge(S.qload, 16)
-    pe.wait_ge(S.c_marg, 2)
+    if is_root:
+        pe.wait_ge(S.qload, 16)
+    else:
+        pe.wait_ge(S.qarr, NE_QC if near else NE_Q)
+    pe.wait_ge(S.c_marg, 3)
     pe.matmul(T.ps_st[0:32, 0:256], T.qz[:, QP:2 * QP], T.kv[:, 0:256], True, True).then_inc(S.s_st, 1)
     pe.matmul(T.ps_s[:, 0:64], T.kv[:, 0:128], T.qz[:, QP:3 * QP], True, False)
     pe.matmul(T.ps_s[:, 0:64], T.kv[:, 128:256], T.qz[:, 0:2 * QP], False, False)
 
+    dve.wait_ge(S.c_marg, 3)
     dve.wait_ge(S.s_st, 1)
-    dve.tensor_reduce(T.negm[0:32, 0:1], T.ps_st[0:32, 0:256], AxisListType.X, AluOpType.max, negate=True
-                      ).then_inc(S.s_m, 1)
+    dve.tensor_reduce(negm, T.ps_st[0:32, 0:256], AxisListType.X, AluOpType.max, negate=True).then_inc(S.s_m, 1)
+    if not is_root:
+        rid, pid, _ = topo.addr(root)
+        em = _engines(topo.mask(core, root), NE_P)
+        g.wait_ge(S.c_marg, 3)
+        g.wait_ge(S.s_m, 1)
+        g.remote_dma(T.mland[:, MS * slot:MS * slot + MS], T.negm[:, :], S.marr, S.sent, pid, rid, em)
     dve.wait_ge(S.s_m, 1)
     dve.wait_ge(S.c_e4, 1)
-    dve.tensor_scalar(T.diag2[0:32, :], T.e4[0:32, 0:64], T.negm[0:32, 0:1], None, AluOpType.mult
-                      ).then_inc(S.s_d, 1)
+    dve.tensor_scalar(T.diag2[0:32, :], T.e4[0:32, 0:64], negm, None, AluOpType.mult).then_inc(S.s_d, 1)
 
-    pe.wait_ge(S.c_e4, 1)
-    pe.wait_ge(S.s_m, 1)
-    pe.matmul(T.ps_m[:, 0:1], T.e4[0:32, :], T.negm[0:32, 0:1], True, True).then_inc(S.s_mr, 1)
     pe.wait_ge(S.c_ones, 1)
     pe.wait_ge(S.s_d, 1)
     pe.matmul(T.ps_s[:, 0:64], T.ones[0:32, :], T.diag2[0:32, :], False, True).then_inc(S.s_s, 1)
-
-    dve.wait_ge(S.s_mr, 1)
-    mdst = T.land[:, slot * SLOT:slot * SLOT + 1] if is_root else T.send[:, 7:8]
-    dve.tensor_copy(mdst, T.ps_m[:, 0:1]).then_inc(S.s_x, 1)
 
     act.wait_ge(S.s_s, 1)
     act.activation(T.p[:, :], T.ps_s[:, 0:64], EXP).then_inc(S.s_p, 1)
 
     pe.wait_ge(S.s_p, 1)
-    if not fed:
+    if fed:
+        pe.wait_ge(S.varr, NE_KV)
+    else:
         pe.wait_ge(S.vload, 16)
     pe.matmul(T.ps_o[:, 0:32], T.kv[:, 256:384], T.p[:, 0:32], True, False)
     pe.matmul(T.ps_o[:, 0:32], T.kv[:, 384:512], T.p[:, 32:64], False, True).then_inc(S.s_o, 1)
@@ -184,51 +190,48 @@ def rank_program(g, core, T, topo):
     dve.wait_ge(S.s_o, 2)
     dve.tensor_copy(T.stg[:, :], T.ps_o[:, 0:64]).then_inc(S.s_g, 1)
     dve.wait_ge(S.s_g, 1)
-    dve.transpose(T.send[:, 8:72], T.stg[:, :]).then_inc(S.s_t, 1)
+    dve.transpose(T.send[:, :], T.stg[:, :]).then_inc(S.s_t, 1)
 
     if not is_root:
-        g.wait_ge(S.s_x, 1)
         g.wait_ge(S.s_t, 1)
-        rid, pid, _ = topo.addr(root)
-        g.remote_dma(T.land[:, slot * SLOT:slot * SLOT + PAY], T.send[:, 7:7 + PAY], S.arrived, S.sent, pid, rid,
-                     _engines(topo.mask(core, root), NE_P))
-        g.wait_ge(S.sent, NE_P)
+        g.remote_dma(T.land[:, slot * SLOT:slot * SLOT + PAY], T.send[:, 0:PAY], S.arrived, S.sent, pid, rid, em)
+        g.wait_ge(S.sent, 2 * NE_P)
         return
 
     total = NE_P * (NR - 1)
-    mview = T.land[:, 0:NR * SLOT:SLOT]
-    dve.wait_ge(S.s_t, 1)
-    dve.wait_ge(S.s_x, 1)
-    dve.wait_ge(S.arrived, total)
-    dve.tensor_reduce(T.nM[:, 0:1], mview, AxisListType.X, AluOpType.min).then_inc(S.r1, 1)
-    act.wait_ge(S.arrived, total)
-    act.wait_ge(S.s_x, 1)
-    act.wait_ge(S.s_t, 1)
+    pe.wait_ge(S.c_e4, 1)
+    pe.wait_ge(S.s_m, 1)
+    pe.wait_ge(S.marr, total)
+    pe.matmul(T.ps_m[:, 0:NR], T.e4[0:32, :], T.mland[0:32, 0:NR * MS:MS], True, True).then_inc(S.r0, 1)
+    dve.wait_ge(S.r0, 1)
+    dve.tensor_reduce(T.nM[:, 0:1], T.ps_m[:, 0:NR], AxisListType.X, AluOpType.min).then_inc(S.r1, 1)
     act.wait_ge(S.r1, 1)
-    act.activation(T.w[:, :], mview, EXP, bias=T.nM[:, 0:1], scale=-1.0).then_inc(S.r2, 1)
+    act.activation(T.w[:, :], T.ps_m[:, 0:NR], EXP, bias=T.nM[:, 0:1], scale=-1.0).then_inc(S.r2, 1)
     dve.wait_ge(S.r2, 1)
+    dve.wait_ge(S.c_id, 1)
     act.wait_ge(S.r2, 1)
-    pe.wait_ge(S.c_id, 1)
-    for i in range(NR // 2):
-        for j in (2 * i, 2 * i + 1):
-            src = T.send[:, 8:41] if j == slot else T.land[:, j * SLOT + 1:j * SLOT + PAY]
-            dst = T.prod[:, 33 * j:33 * j + 33]
-            if j % 2 == 0:
-                dve.tensor_scalar(dst, src, T.w[:, j:j + 1], None, AluOpType.mult).then_inc(S.r3d, 1)
-            else:
-                act.activation(dst, src, COPY, scale=T.w[:, j:j + 1]).then_inc(S.r3a, 1)
-        pe.wait_ge(S.r3d, i + 1)
-        pe.wait_ge(S.r3a, i + 1)
-        mm = pe.matmul(T.ps_y[:, 0:66], T.ident[:, :], T.prod[:, 66 * i:66 * i + 66], i == 0, i == NR // 2 - 1)
+    act.wait_ge(S.c_id, 1)
+    for j in range(NR):
+        dst = T.dg[:, 128 * j:128 * j + 128]
+        if j % 2 == 0:
+            dve.tensor_scalar(dst, T.ident[:, :], T.w[:, j:j + 1], None, AluOpType.mult).then_inc(S.r3d, 1)
+        else:
+            act.activation(dst, T.ident[:, :], COPY, scale=T.w[:, j:j + 1]).then_inc(S.r3a, 1)
+
+    pe.wait_ge(S.s_t, 1)
+    pe.wait_ge(S.arrived, total)
+    for j in range(NR):
+        if j % 2 == 0:
+            pe.wait_ge(S.r3d, j // 2 + 1)
+        else:
+            pe.wait_ge(S.r3a, j // 2 + 1)
+        src = T.send[:, 0:PAY] if j == slot else T.land[:, j * SLOT:j * SLOT + PAY]
+        mm = pe.matmul(T.ps_y[:, 0:PAY], T.dg[:, 128 * j:128 * j + 128], src, j == 0, j == NR - 1)
     mm.then_inc(S.r4, 1)
-    act.wait_ge(S.r4, 1)
-    act.activation(T.hb[:, 0:33], T.ps_y[:, 33:66], COPY).then_inc(S.r5, 1)
-    dve.wait_ge(S.r5, 1)
-    dve.tensor_tensor(T.tot[:, 0:33], T.ps_y[:, 0:33], T.hb[:, 0:33], AluOpType.add).then_inc(S.r6, 1)
-    dve.wait_ge(S.r6, 1)
-    dve.reciprocal(T.rL[:, 0:1], T.tot[:, 32:33]).then_inc(S.r7, 1)
+    dve.wait_ge(S.r4, 1)
+    dve.reciprocal(T.rL[:, 0:1], T.ps_y[:, 32:33]).then_inc(S.r7, 1)
     dve.wait_ge(S.r7, 1)
-    dve.tensor_scalar(T.ysb[:, :], T.tot[:, 0:32], T.rL[:, 0:1], None, AluOpType.mult).then_inc(S.r8, 1)
+    dve.tensor_scalar(T.ysb[:, :], T.ps_y[:, 0:32], T.rL[:, 0:1], None, AluOpType.mult).then_inc(S.r8, 1)
     sy.wait_ge(S.r8, 1)
     act.wait_ge(S.r8, 1)
     for c in range(4):

from concourse.bass import DstId, RemoteDMATransfer
from concourse.mybir import AluOpType, AxisListType, ActivationFunctionType

NSIM = 64
NR = 12
QP = 32
SLOT = 40
PAY = 33
MS = 8
NE_Q = 8
NE_QC = 4
NE_P = 8
NE_KV = 8

SCRATCH = {
    "qd": ("dram", [128, QP], "bfloat16"),
    "qz": ("sbuf", [128, 3 * QP], "bfloat16"),
    "kv": ("sbuf", [128, 512], "bfloat16"),
    "zero": ("sbuf", [128, 128], "bfloat16"),
    "ones": ("sbuf", [128, 128], "bfloat16"),
    "e4": ("sbuf", [128, 128], "bfloat16"),
    "negm": ("sbuf", [128, MS], "bfloat16"),
    "diag2": ("sbuf", [128, 2 * QP], "bfloat16"),
    "p": ("sbuf", [128, 2 * QP], "bfloat16"),
    "stg": ("sbuf", [128, 64], "bfloat16"),
    "send": ("sbuf", [128, 64], "bfloat16"),
    "mland": ("sbuf", [128, NR * MS], "bfloat16"),
    "land": ("sbuf", [128, NR * SLOT], "bfloat16"),
    "ident": ("sbuf", [128, 128], "bfloat16"),
    "dg": ("sbuf", [128, NR * 128], "bfloat16"),
    "nM": ("sbuf", [128, 4], "float32"),
    "w": ("sbuf", [128, NR], "float32"),
    "rL": ("sbuf", [128, 4], "float32"),
    "ysb": ("sbuf", [128, QP], "bfloat16"),
    "ps_st": ("psum", [128, 512], "float32"),
    "ps_s": ("psum", [128, 512], "float32"),
    "ps_m": ("psum", [128, 512], "float32"),
    "ps_o": ("psum", [128, 512], "float32"),
    "ps_y": ("psum", [128, 512], "float32"),
}
SEMAPHORES = ["qstage", "qsent", "qarr", "qload", "kload", "vload", "karr", "varr", "sent", "marr", "arrived",
              "c_zero", "c_marg", "c_ones", "c_e4", "c_id",
              "s_st", "s_m", "s_d", "s_s", "s_p", "s_o", "s_g", "s_t",
              "r0", "r1", "r2", "r3d", "r3a", "r4", "r7", "r8", "yd_s", "yd_a"]

EXP = ActivationFunctionType.Exp
COPY = ActivationFunctionType.Copy


def _engines(mask, n):
    out, k, b = 0, 0, 0
    while k < n:
        if (mask >> b) & 1:
            out |= 1 << b
            k += 1
        b += 1
    return out


def _plan(T, topo):
    root = T.cores[T.root]
    taken = set(T.cores)
    workers, feeds = [], {}
    for c in T.cores:
        if c == root or topo.may_write(c, root):
            workers.append(c)
            continue
        h = [x for x in range(NSIM)
             if x not in taken and topo.chip(x) == topo.chip(c) and topo.may_write(x, root)][0]
        taken.add(h)
        workers.append(h)
        feeds[c] = h
    return root, workers, feeds


def _one_link(topo, a, b):
    return topo.same_plane(topo.chip(a), topo.chip(b)) or topo.mates(topo.chip(a), topo.chip(b))


def rank_program(g, core, T, topo):
    root, workers, feeds = _plan(T, topo)
    S = T.sem
    dve, act, pe, sy = g.vector, g.scalar, g.tensor, g.sync

    if core in feeds:
        h = feeds[core]
        sy.dma_start(T.kv[:, 0:256], T.k[:, :]).then_inc(S.kload, 16)
        act.dma_start(T.kv[:, 256:512], T.v[:, :]).then_inc(S.vload, 16)
        rid, pid, _ = topo.addr(h)
        em = _engines(topo.mask(core, h), NE_KV)
        g.wait_ge(S.kload, 16)
        g.remote_dma(T.kv[:, 0:256], T.kv[:, 0:256], S.karr, S.sent, pid, rid, em)
        g.wait_ge(S.vload, 16)
        g.remote_dma(T.kv[:, 256:512], T.kv[:, 256:512], S.varr, S.sent, pid, rid, em)
        g.wait_ge(S.sent, 2 * NE_KV)
        return
    if core not in workers:
        return

    slot = workers.index(core)
    is_root = core == root
    fed = core in feeds.values()
    near = topo.chip(core) == topo.chip(root)

    dve.memset(T.zero[:, :], 0.0).then_inc(S.c_zero, 1)
    dve.memset(T.qz[:, 0:QP], 0.0).then_inc(S.c_marg, 1)
    dve.memset(T.qz[:, 2 * QP:3 * QP], 0.0).then_inc(S.c_marg, 1)
    dve.memset(T.negm[:, :], 0.0).then_inc(S.c_marg, 1)

    if is_root:
        sy.dma_start(T.qd[:, :], T.q[:, :]).then_inc(S.qstage, 16)
        far_w = sorted([w for w in workers if topo.chip(w) != topo.chip(root)], key=lambda w: _one_link(topo, root, w))
        near_w = [w for w in workers if w != root and topo.chip(w) == topo.chip(root)]
        m_far = topo.mask(root, far_w[0])
        for w in far_w:
            m_far &= topo.mask(root, w)
        m_far = _engines(m_far, NE_Q)
        m_near = _engines(topo.mask(root, near_w[0]) & ~m_far, NE_QC)
        g.wait_ge(S.qstage, 16)
        g.remote_dma_fused([RemoteDMATransfer(
            dst_ids=[DstId(rid=topo.addr(w)[0], pnc=topo.addr(w)[1]) for w in ws],
            dma_engine_mask=m, remote_sem=S.qarr,
            srcs=[T.qd[:, :]], dsts=[T.qz[:, QP:2 * QP] for w in ws], alu_op=0)
            for ws, m in ((far_w, m_far), (near_w, m_near))], local_sem=S.qsent)
        act.wait_ge(S.c_zero, 1)
        act.activation(T.ones[:, :], T.zero[:, :], EXP).then_inc(S.c_ones, 1)
        sy.wait_ge(S.qsent, NE_Q + NE_QC)
        sy.dma_start(T.kv[:, 0:256], T.k[:, :]).then_inc(S.kload, 16)
        act.wait_ge(S.qsent, NE_Q + NE_QC)
        act.dma_start(T.qz[:, QP:2 * QP], T.q[:, :]).then_inc(S.qload, 16)
        act.dma_start(T.kv[:, 256:512], T.v[:, :]).then_inc(S.vload, 16)
    else:
        if not fed:
            sy.dma_start(T.kv[:, 0:256], T.k[:, :]).then_inc(S.kload, 16)
            act.dma_start(T.kv[:, 256:512], T.v[:, :]).then_inc(S.vload, 16)
        act.wait_ge(S.c_zero, 1)
        act.activation(T.ones[:, :], T.zero[:, :], EXP).then_inc(S.c_ones, 1)

    g.wait_ge(S.c_ones, 1)
    g.affine_select(T.e4[0:32, :], T.ones[0:32, :], [[0, 4], [-1, 32]], AluOpType.is_equal, 0.0, 0, 1
                    ).then_inc(S.c_e4, 1)
    if is_root:
        g.affine_select(T.ident[:, :], T.ones[:, :], [[-1, 128]], AluOpType.is_equal, 0.0, 0, 1
                        ).then_inc(S.c_id, 1)

    negm = T.mland[0:32, MS * slot:MS * slot + 1] if is_root else T.negm[0:32, 0:1]
    if fed:
        pe.wait_ge(S.karr, NE_KV)
    else:
        pe.wait_ge(S.kload, 16)
    if is_root:
        pe.wait_ge(S.qload, 16)
    else:
        pe.wait_ge(S.qarr, NE_QC if near else NE_Q)
    pe.wait_ge(S.c_marg, 3)
    pe.matmul(T.ps_st[0:32, 0:256], T.qz[:, QP:2 * QP], T.kv[:, 0:256], True, True).then_inc(S.s_st, 1)
    pe.matmul(T.ps_s[:, 0:64], T.kv[:, 0:128], T.qz[:, QP:3 * QP], True, False)
    pe.matmul(T.ps_s[:, 0:64], T.kv[:, 128:256], T.qz[:, 0:2 * QP], False, False)

    dve.wait_ge(S.c_marg, 3)
    dve.wait_ge(S.s_st, 1)
    dve.tensor_reduce(negm, T.ps_st[0:32, 0:256], AxisListType.X, AluOpType.max, negate=True).then_inc(S.s_m, 1)
    if not is_root:
        rid, pid, _ = topo.addr(root)
        em = _engines(topo.mask(core, root), NE_P)
        g.wait_ge(S.c_marg, 3)
        g.wait_ge(S.s_m, 1)
        g.remote_dma(T.mland[:, MS * slot:MS * slot + MS], T.negm[:, :], S.marr, S.sent, pid, rid, em)
    dve.wait_ge(S.s_m, 1)
    dve.wait_ge(S.c_e4, 1)
    dve.tensor_scalar(T.diag2[0:32, :], T.e4[0:32, 0:64], negm, None, AluOpType.mult).then_inc(S.s_d, 1)

    pe.wait_ge(S.c_ones, 1)
    pe.wait_ge(S.s_d, 1)
    pe.matmul(T.ps_s[:, 0:64], T.ones[0:32, :], T.diag2[0:32, :], False, True).then_inc(S.s_s, 1)

    act.wait_ge(S.s_s, 1)
    act.activation(T.p[:, :], T.ps_s[:, 0:64], EXP).then_inc(S.s_p, 1)

    pe.wait_ge(S.s_p, 1)
    if fed:
        pe.wait_ge(S.varr, NE_KV)
    else:
        pe.wait_ge(S.vload, 16)
    pe.matmul(T.ps_o[:, 0:32], T.kv[:, 256:384], T.p[:, 0:32], True, False)
    pe.matmul(T.ps_o[:, 0:32], T.kv[:, 384:512], T.p[:, 32:64], False, True).then_inc(S.s_o, 1)
    pe.matmul(T.ps_o[:, 32:64], T.ones[:, :], T.p[:, 0:32], True, False)
    pe.matmul(T.ps_o[:, 32:64], T.ones[:, :], T.p[:, 32:64], False, True).then_inc(S.s_o, 1)

    dve.wait_ge(S.s_o, 2)
    dve.tensor_copy(T.stg[:, :], T.ps_o[:, 0:64]).then_inc(S.s_g, 1)
    dve.wait_ge(S.s_g, 1)
    dve.transpose(T.send[:, :], T.stg[:, :]).then_inc(S.s_t, 1)

    if not is_root:
        g.wait_ge(S.s_t, 1)
        g.remote_dma(T.land[:, slot * SLOT:slot * SLOT + PAY], T.send[:, 0:PAY], S.arrived, S.sent, pid, rid, em)
        g.wait_ge(S.sent, 2 * NE_P)
        return

    total = NE_P * (NR - 1)
    pe.wait_ge(S.c_e4, 1)
    pe.wait_ge(S.s_m, 1)
    pe.wait_ge(S.marr, total)
    pe.matmul(T.ps_m[:, 0:NR], T.e4[0:32, :], T.mland[0:32, 0:NR * MS:MS], True, True).then_inc(S.r0, 1)
    dve.wait_ge(S.r0, 1)
    dve.tensor_reduce(T.nM[:, 0:1], T.ps_m[:, 0:NR], AxisListType.X, AluOpType.min).then_inc(S.r1, 1)
    act.wait_ge(S.r1, 1)
    act.activation(T.w[:, :], T.ps_m[:, 0:NR], EXP, bias=T.nM[:, 0:1], scale=-1.0).then_inc(S.r2, 1)
    dve.wait_ge(S.r2, 1)
    dve.wait_ge(S.c_id, 1)
    act.wait_ge(S.r2, 1)
    act.wait_ge(S.c_id, 1)
    for j in range(NR):
        dst = T.dg[:, 128 * j:128 * j + 128]
        if j % 2 == 0:
            dve.tensor_scalar(dst, T.ident[:, :], T.w[:, j:j + 1], None, AluOpType.mult).then_inc(S.r3d, 1)
        else:
            act.activation(dst, T.ident[:, :], COPY, scale=T.w[:, j:j + 1]).then_inc(S.r3a, 1)

    pe.wait_ge(S.s_t, 1)
    pe.wait_ge(S.arrived, total)
    for j in range(NR):
        if j % 2 == 0:
            pe.wait_ge(S.r3d, j // 2 + 1)
        else:
            pe.wait_ge(S.r3a, j // 2 + 1)
        src = T.send[:, 0:PAY] if j == slot else T.land[:, j * SLOT:j * SLOT + PAY]
        mm = pe.matmul(T.ps_y[:, 0:PAY], T.dg[:, 128 * j:128 * j + 128], src, j == 0, j == NR - 1)
    mm.then_inc(S.r4, 1)
    dve.wait_ge(S.r4, 1)
    dve.reciprocal(T.rL[:, 0:1], T.ps_y[:, 32:33]).then_inc(S.r7, 1)
    dve.wait_ge(S.r7, 1)
    dve.tensor_scalar(T.ysb[:, :], T.ps_y[:, 0:32], T.rL[:, 0:1], None, AluOpType.mult).then_inc(S.r8, 1)
    sy.wait_ge(S.r8, 1)
    act.wait_ge(S.r8, 1)
    for c in range(4):
        q_, s_ = (sy, S.yd_s) if c % 2 == 0 else (act, S.yd_a)
        q_.dma_start(T.y[:, 32 * c:32 * c + 32], T.ysb[32 * c:32 * c + 32, :]).then_inc(s_, 16)
    sy.wait_ge(S.yd_s, 32)
    act.wait_ge(S.yd_a, 32)
